import numpy as np
import ml_dtypes


def mxq(x, axis, fmt="e4m3"):
    dtype, down = {"e4m3": (ml_dtypes.float8_e4m3fn, 7), "e5m2": (ml_dtypes.float8_e5m2, 14)}[fmt]
    v = np.moveaxis(np.asarray(x, np.float32).astype(ml_dtypes.bfloat16).astype(np.float64), axis, -1)
    blocks = v.reshape(v.shape[:-1] + (-1, 32))
    amax = np.abs(blocks).max(-1, keepdims=True)
    byte = np.maximum(np.where(amax > 0, np.frexp(amax)[1] - 1 + 127, 0) - down, 1)
    scale = np.exp2(byte - 127.0)
    codes = (blocks / scale).astype(np.float32).astype(dtype).astype(np.float64)
    return np.moveaxis((codes * scale).reshape(v.shape), -1, axis)


WIDE = False


def mx_kscale(k):
    if not WIDE:
        return np.ones(k)
    levels = np.array([30, -30])
    if k % 512:
        return np.exp2(np.random.permutation(np.resize(levels, k // 32))).repeat(32)
    a = np.empty((k // 512, 16))
    for p in range(k // 512):
        a[p, :8] = np.random.permutation(np.resize(levels, 8))
        for g in range(8):
            far = levels[np.abs(levels - a[p, g]) >= 10]
            a[p, g + 8] = far[np.random.randint(len(far))]
    return np.exp2(a.ravel()).repeat(32)


def f64(x):
    return np.asarray(x).astype(np.float64)


def striped(idx):
    return np.tile(np.asarray(idx).reshape(-1, 16).T, (8, 1)).astype(np.uint16)


def unstriped(offs):
    return offs[:16].T.reshape(-1).astype(np.int64)


E2M1 = np.array([0.0, 0.5, 1.0, 1.5, 2.0, 3.0, 4.0, 6.0, -0.0, -0.5, -1.0, -1.5, -2.0, -3.0, -4.0, -6.0])


def pack_weight(w, fmt):
    k, n = w.shape
    w = f64(np.asarray(w, np.float32).astype(ml_dtypes.bfloat16)).reshape(k // 32, 32, n)
    amax = np.abs(w).max(1)
    if fmt in ("e4m3", "e5m2"):
        byte = np.frexp(amax)[1] - 1 + 127 - (7 if fmt == "e4m3" else 14)
    else:
        mant, ex = np.frexp(amax / 6.0)
        byte = np.where(mant > 0.5, ex, ex - 1) + 127
    byte = np.clip(np.where(amax > 0, byte, 1), 1, 254)
    scaled = (w * np.exp2(127.0 - byte)[:, None, :]).reshape(k, n).astype(np.float32)
    by_word = np.ascontiguousarray(scaled.reshape(k // 512, 128, 4, n).transpose(0, 1, 3, 2))
    if fmt in ("e4m3", "e5m2"):
        words = by_word.astype(ml_dtypes.float8_e4m3fn if fmt == "e4m3" else ml_dtypes.float8_e5m2).view(np.uint8)
    else:
        c = by_word.astype(ml_dtypes.float4_e2m1fn).view(np.uint8) & 0xF
        words = (c[..., 0::2] | (c[..., 1::2] << 4)).reshape(k // 512, 128, 2 * n)
    return np.ascontiguousarray(words), np.ascontiguousarray(byte.astype(np.uint8).reshape(k // 512, 16, n))


def unpack_weight(words, scales, fmt):
    g, _, n = scales.shape
    words = np.ascontiguousarray(words).reshape(g, 128, n, -1)
    if fmt in ("e4m3", "e5m2"):
        vals = words.view(ml_dtypes.float8_e4m3fn if fmt == "e4m3" else ml_dtypes.float8_e5m2).astype(np.float64)
    else:
        nib = np.empty((g, 128, n, 4), np.uint8)
        nib[..., 0::2] = words & 0xF
        nib[..., 1::2] = words >> 4
        vals = E2M1[nib]
    vals = vals * np.repeat(np.exp2(scales.astype(np.float64) - 127.0), 8, axis=1)[..., None]
    return vals.transpose(0, 1, 3, 2).reshape(g * 512, n)


K, T, J, I, R, C, S = 512, 512, 256, 256, 512, 512, 32


def setup_inputs():
    n = np.random.standard_normal
    idx = np.random.permutation(T)[:J]
    idx2 = np.random.permutation(C)[:J]
    idx3 = np.random.permutation(T)[:I]
    fk = mx_kscale(K)
    fr = mx_kscale(R)
    xtp = pack_weight(n((K, T)) / fk[:, None], "e4m3")
    wap = pack_weight(n((K, R)) * 0.5 / np.sqrt(K) * fk[:, None] * fr, "e2m1")
    wbp = pack_weight(n((K, R)) * 1 / np.sqrt(K) * fk[:, None] / fr, "e5m2")
    return {
        "xt_words": xtp[0],
        "xt_scales": xtp[1],
        "wa_words": wap[0],
        "wa_scales": wap[1],
        "tf": (n((R, C))).astype(np.float32),
        "wb_words": wbp[0],
        "wb_scales": wbp[1],
        "ob": (n((R, I)) * 0.5 / fr[:, None]).astype(np.float32),
        "bi": (np.random.uniform(-15.0, 15.0, (1, I))).astype(np.float32),
        "offs": striped(idx),
        "offs2": striped(idx2),
        "offs3": striped(idx3),
    }


def reference(xt_words, xt_scales, wa_words, wa_scales, tf, wb_words, wb_scales, ob, bi, offs, offs2, offs3):
    idx = unstriped(offs)
    idx2 = unstriped(offs2)
    idx3 = unstriped(offs3)
    xtu = unpack_weight(xt_words, xt_scales, "e4m3")
    wau = unpack_weight(wa_words, wa_scales, "e2m1")
    wbu = unpack_weight(wb_words, wb_scales, "e5m2")
    xtidxg = xtu[:, idx]
    za = wau.T @ xtidxg
    ha = za * f64(tf)[:, idx2]
    xtidx3g = xtu[:, idx3]
    zb = wbu.T @ xtidx3g
    hb = np.maximum(zb, f64(ob))
    haq = mxq(ha, 0, "e4m3")
    hbq = mxq(hb, 0, "e5m2")
    a0 = haq.T @ hbq
    a = a0 + f64(bi)
    g1 = a.reshape(J, S, I // S).max(axis=2)
    y = 0.04 * g1
    return y

@@ -1,0 +1,186 @@
+from contextlib import ExitStack
+
+import concourse.mybir as mybir
+from concourse.masks import make_identity
+
+K, T, J, I, R, C, S = 512, 512, 256, 256, 512, 512, 32
+FLOPS = 2 * K * R * J + 2 * K * R * I + 2 * R * J * I
+
+F32 = mybir.dt.float32
+BF16 = mybir.dt.bfloat16
+I32 = mybir.dt.int32
+U32 = mybir.dt.uint32
+U16 = mybir.dt.uint16
+U8 = mybir.dt.uint8
+E4M3 = mybir.dt.float8_e4m3fn_x4
+E5M2 = mybir.dt.float8_e5m2_x4
+E2M1 = mybir.dt.float4_e2m1fn_x4
+MULT = mybir.AluOpType.mult
+ADD = mybir.AluOpType.add
+MAX = mybir.AluOpType.max
+COPY = mybir.ActivationFunctionType.Copy
+
+P = 128
+PACK = 4
+HALF = 128
+OUT_SCALE = 0.04
+
+
+def tile_list_meet_timestable_added_bundlemax_kernel(
+    tc, xt_words, xt_scales, wa_words, wa_scales, tf, wb_words, wb_scales, ob, bi, offs, offs2, offs3, out
+):
+    nc = tc.nc
+    with ExitStack() as ctx:
+        lists = ctx.enter_context(tc.tile_pool(name="lists", bufs=1))
+        sb = ctx.enter_context(tc.tile_pool(name="sb", bufs=1))
+        ps = ctx.enter_context(tc.psum_pool(name="ps", bufs=1))
+
+        list_a = lists.tile([P, J // 16], U16, name="list_a")
+        list_f = lists.tile([P, J // 16], U16, name="list_f")
+        list_b = lists.tile([P, I // 16], U16, name="list_b")
+
+        def tile(name, shape, dtype, tag=None):
+            return sb.tile(shape, dtype, name=name, tag=tag or name, align_bytes=64)
+
+        xw = tile("xw", [P, T], U32)
+        xs = tile("xs", [P, T], U8)
+        wa_raw = tile("wa_raw", [P, R], U16)
+        was_raw = tile("was_raw", [P, R], U8)
+        wb_raw = tile("wb_raw", [P, R], U32)
+        wbs_raw = tile("wbs_raw", [P, R], U8)
+        tf_lo = tile("tf_lo", [P, 2, C], F32)
+        tf_hi = tile("tf_hi", [P, 2, C], F32)
+        ob_sb = tile("ob_sb", [P, PACK, I], F32)
+        bi_col = tile("bi_col", [P, 2], F32)
+        ident = tile("ident", [P, P], F32)
+
+        for plane in (xs, was_raw, wbs_raw):
+            nc.vector.memset(plane[:].bitcast(I32), 0)
+
+        def load_scales(queue, plane, scales, q):
+            queue.dma_start(plane[32 * q : 32 * q + 4, :].bitcast(I32), scales[0, 4 * q : 4 * q + 4, :].bitcast(I32))
+
+        tf_rows = tf.rearrange("(p t) c -> p t c", t=PACK)
+        nc.sync.dma_start(list_a[:], offs)
+        nc.scalar.dma_start(wa_raw[:].bitcast(I32), wa_words[0].bitcast(I32))
+        nc.sync.dma_start(xw[:].bitcast(I32), xt_words[0].rearrange("p n t -> p (n t)").bitcast(I32))
+        load_scales(nc.scalar, xs, xt_scales, 2)
+        load_scales(nc.sync, xs, xt_scales, 0)
+        load_scales(nc.scalar, xs, xt_scales, 3)
+        load_scales(nc.sync, xs, xt_scales, 1)
+        nc.scalar.dma_start(tf_lo[:], tf_rows[:, 0:2, :])
+        nc.gpsimd.dma_start(tf_hi[:], tf_rows[:, 2:4, :])
+        nc.gpsimd.dma_start(ob_sb[:], ob.rearrange("(p t) i -> p t i", t=PACK))
+        nc.gpsimd.dma_start(bi_col[:], bi.rearrange("o (p c) -> p (o c)", c=2))
+        nc.sync.dma_start(list_b[:], offs3)
+        for q in range(4):
+            load_scales(nc.sync, was_raw, wa_scales, q)
+        nc.sync.dma_start(list_f[:], offs2)
+        nc.sync.dma_start(wb_raw[:].bitcast(I32), wb_words[0].rearrange("p n t -> p (n t)").bitcast(I32))
+        for q in range(4):
+            load_scales(nc.sync, wbs_raw, wb_scales, q)
+        make_identity(nc, ident[:])
+
+        def gather_tokens(name, offsets, n):
+            words = tile(name + "_w", [P, n], U32)
+            scales = tile(name + "_s", [P, n], U8)
+            nc.vector.tensor_copy(words[:], xw[:].indirect(offsets[:]))
+            nc.vector.tensor_copy(scales[:], xs[:].indirect(offsets[:]))
+            return words, scales
+
+        def deal(name, raw, dtype, run):
+            dealt = tile(name, [P, R], dtype)
+            nc.vector.tensor_copy(
+                dealt[:].rearrange("p (t c i) -> p c t i", t=PACK, i=run),
+                raw[:].rearrange("p (c i t) -> p c t i", t=PACK, i=run),
+            )
+            return dealt
+
+        def first_product(name, w_words, w_dtype, w_scales, x_words, x_scales):
+            banks = []
+            for h in range(2):
+                bank = ps.tile([P, PACK, HALF], F32, name=f"{name}{h}")
+                cols = slice(h * HALF, (h + 1) * HALF)
+                for t in range(PACK):
+                    rows = slice(t * P, (t + 1) * P)
+                    nc.tensor.matmul_mx(
+                        out=bank[:, t, :],
+                        lhsT=w_words[:, rows].bitcast(w_dtype),
+                        lhsT_scale=w_scales[:, rows],
+                        rhs=x_words[:, cols].bitcast(E4M3),
+                        rhs_scale=x_scales[:, cols],
+                        start=True,
+                        stop=True,
+                    )
+                banks.append(bank)
+            return banks
+
+        xa_w, xa_s = gather_tokens("xa", list_a, J)
+        wa_w = deal("wa_w", wa_raw, U16, 8)
+        wa_s = deal("wa_s", was_raw, U8, 16)
+        za = first_product("za", wa_w, E2M1, wa_s, xa_w, xa_s)
+        xb_w, xb_s = gather_tokens("xb", list_b, I)
+        wb_w = deal("wb_w", wb_raw, U32, 4)
+        wb_s = deal("wb_s", wbs_raw, U8, 16)
+        zb = first_product("zb", wb_w, E5M2, wb_s, xb_w, xb_s)
+
+        tfg = [tile(f"tfg{h}", [P, PACK, HALF], F32) for h in range(2)]
+        for h in range(2):
+            for pair, rows in enumerate((tf_lo, tf_hi)):
+                for u in range(2):
+                    nc.scalar.activation(
+                        tfg[h][:, 2 * pair + u, :], rows[:, u, :].indirect(list_f[:, 8 * h : 8 * h + 8]), COPY
+                    )
+
+        bias_ps = ps.tile([P, 2, P], F32, name="bias_ps")
+        for c in range(2):
+            nc.tensor.transpose(bias_ps[:, c, :], bi_col[:, c : c + 1].to_broadcast([P, P]), ident[:])
+        bias = tile("bias", [P, I], F32)
+        nc.scalar.activation(
+            bias[:].rearrange("p (n c) -> p n c", c=2), bias_ps[:].rearrange("p c n -> p n c"), COPY, scale=OUT_SCALE
+        )
+
+        def combine(dst, bank, other, op):
+            nc.vector.tensor_tensor(
+                dst.rearrange("p (c i t) -> p c t i", t=PACK, i=4),
+                bank[:].rearrange("p t (c i) -> p c t i", i=4),
+                other.rearrange("p t (c i) -> p c t i", i=4),
+                op,
+            )
+
+        ha = [tile("ha0", [P, HALF * PACK], BF16, tag="wbs_raw"), tile("ha1", [P, HALF * PACK], BF16)]
+        hb = [tile(f"hb{h}", [P, HALF * PACK], BF16) for h in range(2)]
+        ha_w = [tile(f"ha_w{h}", [P, HALF], U32) for h in range(2)]
+        ha_s = [tile(f"ha_s{h}", [P, HALF], U8) for h in range(2)]
+        hb_w = tile("hb_w", [P, I], U32)
+        hb_s = tile("hb_s", [P, I], U8)
+        for h in range(2):
+            combine(ha[h][:], za[h], tfg[h][:], MULT)
+        for h in range(2):
+            combine(hb[h][:], zb[h], ob_sb[:, :, h * HALF : (h + 1) * HALF], MAX)
+            nc.vector.quantize_mx(out=ha_w[h][:].bitcast(E4M3), scales=ha_s[h][:], in_=ha[h][:])
+        for h in range(2):
+            cols = slice(h * HALF, (h + 1) * HALF)
+            nc.vector.quantize_mx(out=hb_w[:, cols].bitcast(E5M2), scales=hb_s[:, cols], in_=hb[h][:])
+
+        scores = []
+        for h in range(2):
+            bank = ps.tile([P, I], F32, name=f"a0_{h}")
+            nc.tensor.matmul_mx(
+                out=bank[:],
+                lhsT=ha_w[h][:].bitcast(E4M3),
+                lhsT_scale=ha_s[h][:],
+                rhs=hb_w[:].bitcast(E5M2),
+                rhs_scale=hb_s[:],
+                start=True,
+                stop=True,
+            )
+            scored = tile(f"scored{h}", [P, I], F32)
+            nc.vector.scalar_tensor_tensor(scored[:], bank[:], OUT_SCALE, bias[:], MULT, ADD)
+            scores.append(scored)
+        for h in range(2):
+            best = tile(f"best{h}", [P, S], F32)
+            nc.vector.tensor_reduce(
+                best[:], scores[h][:].rearrange("p (s e) -> p s e", s=S), mybir.AxisListType.X, MAX
+            )
+            (nc.sync, nc.scalar)[h].dma_start(out[h * HALF : (h + 1) * HALF, :], best[:])

@@ -1,7 +1,6 @@
 from contextlib import ExitStack
 
 import concourse.mybir as mybir
-from concourse.masks import make_identity
 
 K, T, J, I, R, C, S = 512, 512, 256, 256, 512, 512, 32
 FLOPS = 2 * K * R * J + 2 * K * R * I + 2 * R * J * I
@@ -51,35 +50,37 @@ def tile_list_meet_timestable_added_bundlemax_kernel(
         tf_lo = tile("tf_lo", [P, 2, C], F32)
         tf_hi = tile("tf_hi", [P, 2, C], F32)
         ob_sb = tile("ob_sb", [P, PACK, I], F32)
-        bi_col = tile("bi_col", [P, 2], F32)
-        ident = tile("ident", [P, P], F32)
+        bi_sb = tile("bi_sb", [P, I], F32)
 
-        for plane in (xs, was_raw, wbs_raw):
-            nc.vector.memset(plane[:].bitcast(I32), 0)
+        def load_scales_quadrant(queue, plane, scales, q):
+            rows = scales[0, 4 * q : 4 * q + 4, :].bitcast(I32)
+            queue.dma_start(plane[32 * q : 32 * q + 32, :].bitcast(I32), rows.unsqueeze(0).broadcast_to([8, 4, R // 4]))
 
-        def load_scales(queue, plane, scales, q):
-            queue.dma_start(plane[32 * q : 32 * q + 4, :].bitcast(I32), scales[0, 4 * q : 4 * q + 4, :].bitcast(I32))
+        def load_scales_low(queue, plane, scales):
+            rows = scales[0, 0:4, :].bitcast(I32)
+            queue.dma_start(plane[0:16, :].bitcast(I32), rows.unsqueeze(0).broadcast_to([4, 4, R // 4]))
+
+        def load_scales_high(queue, plane, scales):
+            rows = scales[0, 2:16, :].bitcast(I32)
+            queue.dma_start(plane[16:P, :].bitcast(I32), rows.unsqueeze(0).broadcast_to([8, 14, R // 4]))
 
         tf_rows = tf.rearrange("(p t) c -> p t c", t=PACK)
-        nc.sync.dma_start(list_a[:], offs)
-        nc.scalar.dma_start(wa_raw[:].bitcast(I32), wa_words[0].bitcast(I32))
-        nc.sync.dma_start(xw[:].bitcast(I32), xt_words[0].rearrange("p n t -> p (n t)").bitcast(I32))
-        load_scales(nc.scalar, xs, xt_scales, 2)
-        load_scales(nc.sync, xs, xt_scales, 0)
-        load_scales(nc.scalar, xs, xt_scales, 3)
-        load_scales(nc.sync, xs, xt_scales, 1)
-        nc.scalar.dma_start(tf_lo[:], tf_rows[:, 0:2, :])
-        nc.gpsimd.dma_start(tf_hi[:], tf_rows[:, 2:4, :])
-        nc.gpsimd.dma_start(ob_sb[:], ob.rearrange("(p t) i -> p t i", t=PACK))
-        nc.gpsimd.dma_start(bi_col[:], bi.rearrange("o (p c) -> p (o c)", c=2))
+        for q in range(4):
+            load_scales_quadrant(nc.scalar, xs, xt_scales, q)
         nc.sync.dma_start(list_b[:], offs3)
-        for q in range(4):
-            load_scales(nc.sync, was_raw, wa_scales, q)
-        nc.sync.dma_start(list_f[:], offs2)
+        nc.sync.dma_start(list_a[:], offs)
+        nc.sync.dma_start(xw[:].bitcast(I32), xt_words[0].rearrange("p n t -> p (n t)").bitcast(I32))
+        nc.sync.dma_start(ob_sb[:], ob.rearrange("(p t) i -> p t i", t=PACK))
+        load_scales_low(nc.sync, wbs_raw, wb_scales)
         nc.sync.dma_start(wb_raw[:].bitcast(I32), wb_words[0].rearrange("p n t -> p (n t)").bitcast(I32))
-        for q in range(4):
-            load_scales(nc.sync, wbs_raw, wb_scales, q)
-        make_identity(nc, ident[:])
+        nc.sync.dma_start(wa_raw[:].bitcast(I32), wa_words[0].bitcast(I32))
+        nc.sync.dma_start(tf_lo[:], tf_rows[:, 0:2, :])
+        nc.sync.dma_start(list_f[:], offs2)
+        load_scales_high(nc.sync, was_raw, wa_scales)
+        nc.sync.dma_start(tf_hi[:], tf_rows[:, 2:4, :])
+        nc.sync.dma_start(bi_sb[:], bi[0].partition_broadcast(P))
+        load_scales_high(nc.gpsimd, wbs_raw, wb_scales)
+        load_scales_low(nc.gpsimd, was_raw, wa_scales)
 
         def gather_tokens(name, offsets, n):
             words = tile(name + "_w", [P, n], U32)
@@ -88,9 +89,9 @@ def tile_list_meet_timestable_added_bundlemax_kernel(
             nc.vector.tensor_copy(scales[:], xs[:].indirect(offsets[:]))
             return words, scales
 
-        def deal(name, raw, dtype, run):
-            dealt = tile(name, [P, R], dtype)
-            nc.vector.tensor_copy(
+        def deal(copy, name, raw, dtype, run, tag=None):
+            dealt = tile(name, [P, R], dtype, tag)
+            copy(
                 dealt[:].rearrange("p (t c i) -> p c t i", t=PACK, i=run),
                 raw[:].rearrange("p (c i t) -> p c t i", t=PACK, i=run),
             )
@@ -115,30 +116,25 @@ def tile_list_meet_timestable_added_bundlemax_kernel(
                 banks.append(bank)
             return banks
 
-        xa_w, xa_s = gather_tokens("xa", list_a, J)
-        wa_w = deal("wa_w", wa_raw, U16, 8)
-        wa_s = deal("wa_s", was_raw, U8, 16)
-        za = first_product("za", wa_w, E2M1, wa_s, xa_w, xa_s)
         xb_w, xb_s = gather_tokens("xb", list_b, I)
-        wb_w = deal("wb_w", wb_raw, U32, 4)
-        wb_s = deal("wb_s", wbs_raw, U8, 16)
+        xa_w, xa_s = gather_tokens("xa", list_a, J)
+        wb_s = deal(nc.vector.tensor_copy, "wb_s", wbs_raw, U8, 16)
+        wb_w = deal(nc.scalar.copy, "wb_w", wb_raw, U32, 4)
         zb = first_product("zb", wb_w, E5M2, wb_s, xb_w, xb_s)
+        wa_s = deal(nc.vector.tensor_copy, "wa_s", was_raw, U8, 16)
+        wa_w = deal(nc.scalar.copy, "wa_w", wa_raw, U16, 8)
+        za = first_product("za", wa_w, E2M1, wa_s, xa_w, xa_s)
 
         tfg = [tile(f"tfg{h}", [P, PACK, HALF], F32) for h in range(2)]
-        for h in range(2):
-            for pair, rows in enumerate((tf_lo, tf_hi)):
+        for pair, rows in enumerate((tf_lo, tf_hi)):
+            for h in range(2):
                 for u in range(2):
                     nc.scalar.activation(
                         tfg[h][:, 2 * pair + u, :], rows[:, u, :].indirect(list_f[:, 8 * h : 8 * h + 8]), COPY
                     )
 
-        bias_ps = ps.tile([P, 2, P], F32, name="bias_ps")
-        for c in range(2):
-            nc.tensor.transpose(bias_ps[:, c, :], bi_col[:, c : c + 1].to_broadcast([P, P]), ident[:])
         bias = tile("bias", [P, I], F32)
-        nc.scalar.activation(
-            bias[:].rearrange("p (n c) -> p n c", c=2), bias_ps[:].rearrange("p c n -> p n c"), COPY, scale=OUT_SCALE
-        )
+        nc.scalar.activation(bias[:], bi_sb[:], COPY, scale=OUT_SCALE)
 
         def combine(dst, bank, other, op):
             nc.vector.tensor_tensor(
@@ -148,20 +144,21 @@ def tile_list_meet_timestable_added_bundlemax_kernel(
                 op,
             )
 
-        ha = [tile("ha0", [P, HALF * PACK], BF16, tag="wbs_raw"), tile("ha1", [P, HALF * PACK], BF16)]
-        hb = [tile(f"hb{h}", [P, HALF * PACK], BF16) for h in range(2)]
+        ha = [tile(f"ha{h}", [P, HALF * PACK], BF16) for h in range(2)]
+        hb = [tile("hb0", [P, HALF * PACK], BF16), tile("hb1", [P, HALF * PACK], BF16, tag="was_raw")]
         ha_w = [tile(f"ha_w{h}", [P, HALF], U32) for h in range(2)]
         ha_s = [tile(f"ha_s{h}", [P, HALF], U8) for h in range(2)]
         hb_w = tile("hb_w", [P, I], U32)
         hb_s = tile("hb_s", [P, I], U8)
         for h in range(2):
-            combine(ha[h][:], za[h], tfg[h][:], MULT)
-        for h in range(2):
             combine(hb[h][:], zb[h], ob_sb[:, :, h * HALF : (h + 1) * HALF], MAX)
-            nc.vector.quantize_mx(out=ha_w[h][:].bitcast(E4M3), scales=ha_s[h][:], in_=ha[h][:])
         for h in range(2):
             cols = slice(h * HALF, (h + 1) * HALF)
             nc.vector.quantize_mx(out=hb_w[:, cols].bitcast(E5M2), scales=hb_s[:, cols], in_=hb[h][:])
+        for h in range(2):
+            combine(ha[h][:], za[h], tfg[h][:], MULT)
+        for h in range(2):
+            nc.vector.quantize_mx(out=ha_w[h][:].bitcast(E4M3), scales=ha_s[h][:], in_=ha[h][:])
 
         scores = []
         for h in range(2):

@@ -50,7 +50,7 @@ def tile_list_meet_timestable_added_bundlemax_kernel(
         tf_lo = tile("tf_lo", [P, 2, C], F32)
         tf_hi = tile("tf_hi", [P, 2, C], F32)
         ob_sb = tile("ob_sb", [P, PACK, I], F32)
-        bi_sb = tile("bi_sb", [P, I], F32)
+        bi_col = tile("bi_col", [P, 2], F32)
 
         def load_scales_quadrant(queue, plane, scales, q):
             rows = scales[0, 4 * q : 4 * q + 4, :].bitcast(I32)
@@ -78,9 +78,21 @@ def tile_list_meet_timestable_added_bundlemax_kernel(
         nc.sync.dma_start(list_f[:], offs2)
         load_scales_high(nc.sync, was_raw, wa_scales)
         nc.sync.dma_start(tf_hi[:], tf_rows[:, 2:4, :])
-        nc.sync.dma_start(bi_sb[:], bi[0].partition_broadcast(P))
+        nc.sync.dma_start(bi_col[:], bi.rearrange("o (p c) -> p (o c)", c=2))
         load_scales_high(nc.gpsimd, wbs_raw, wb_scales)
         load_scales_low(nc.gpsimd, was_raw, wa_scales)
+
+        ones = tile("ones", [P, 32], F32)
+        column = tile("column", [P, 32], F32)
+        row = tile("row", [P, 32], F32)
+        ident = tile("ident", [P, P], F32)
+        nc.vector.memset(ones[:], 1.0)
+        nc.vector.memset(ident[:], 0.0)
+        nc.vector.tensor_tensor_scan(column[:], ones[:], ones[:], 0.0, MULT, ADD)
+        nc.vector.transpose(row[:], column[:])
+        for q in range(4):
+            block = slice(32 * q, 32 * q + 32)
+            nc.vector.tensor_tensor(ident[block, block], column[block, :], row[block, :], mybir.AluOpType.is_equal)
 
         def gather_tokens(name, offsets, n):
             words = tile(name + "_w", [P, n], U32)
@@ -133,14 +145,19 @@ def tile_list_meet_timestable_added_bundlemax_kernel(
                         tfg[h][:, 2 * pair + u, :], rows[:, u, :].indirect(list_f[:, 8 * h : 8 * h + 8]), COPY
                     )
 
+        bias_ps = ps.tile([P, 2, P], F32, name="bias_ps")
+        for c in range(2):
+            nc.tensor.transpose(bias_ps[:, c, :], bi_col[:, c : c + 1].to_broadcast([P, P]), ident[:])
         bias = tile("bias", [P, I], F32)
-        nc.scalar.activation(bias[:], bi_sb[:], COPY, scale=OUT_SCALE)
+        nc.scalar.activation(
+            bias[:].rearrange("p (n c) -> p n c", c=2), bias_ps[:].rearrange("p c n -> p n c"), COPY, scale=OUT_SCALE
+        )
 
         def combine(dst, bank, other, op):
             nc.vector.tensor_tensor(
-                dst.rearrange("p (c i t) -> p c t i", t=PACK, i=4),
-                bank[:].rearrange("p t (c i) -> p c t i", i=4),
-                other.rearrange("p t (c i) -> p c t i", i=4),
+                dst.rearrange("p (c i t) -> p c t i", t=PACK, i=2),
+                bank[:].rearrange("p t (c i) -> p c t i", i=2),
+                other.rearrange("p t (c i) -> p c t i", i=2),
                 op,
             )
 

@@ -48,13 +48,10 @@ def tile_list_meet_timestable_added_bundlemax_kernel(
         wb_raw = tile("wb_raw", [P, R], U32)
         wbs_raw = tile("wbs_raw", [P, R], U8)
         tf_lo = tile("tf_lo", [P, 2, C], F32)
-        tf_hi = tile("tf_hi", [P, 2, C], F32)
+        tf_mid = tile("tf_mid", [P, C], F32)
+        tf_hi = tile("tf_hi", [P, C], F32)
         ob_sb = tile("ob_sb", [P, PACK, I], F32)
         bi_col = tile("bi_col", [P, 2], F32)
-
-        def load_scales_quadrant(queue, plane, scales, q):
-            rows = scales[0, 4 * q : 4 * q + 4, :].bitcast(I32)
-            queue.dma_start(plane[32 * q : 32 * q + 32, :].bitcast(I32), rows.unsqueeze(0).broadcast_to([8, 4, R // 4]))
 
         def load_scales_low(queue, plane, scales):
             rows = scales[0, 0:4, :].bitcast(I32)
@@ -65,22 +62,23 @@ def tile_list_meet_timestable_added_bundlemax_kernel(
             queue.dma_start(plane[16:P, :].bitcast(I32), rows.unsqueeze(0).broadcast_to([8, 14, R // 4]))
 
         tf_rows = tf.rearrange("(p t) c -> p t c", t=PACK)
-        for q in range(4):
-            load_scales_quadrant(nc.scalar, xs, xt_scales, q)
+        load_scales_low(nc.scalar, was_raw, wa_scales)
+        load_scales_high(nc.scalar, xs, xt_scales)
+        nc.scalar.dma_start(wb_raw[:].bitcast(I32), wb_words[0].rearrange("p n t -> p (n t)").bitcast(I32))
+        nc.scalar.dma_start(tf_lo[:], tf_rows[:, 0:2, :])
         nc.sync.dma_start(list_b[:], offs3)
-        nc.sync.dma_start(list_a[:], offs)
         nc.sync.dma_start(xw[:].bitcast(I32), xt_words[0].rearrange("p n t -> p (n t)").bitcast(I32))
-        nc.sync.dma_start(ob_sb[:], ob.rearrange("(p t) i -> p t i", t=PACK))
+        load_scales_low(nc.sync, xs, xt_scales)
         load_scales_low(nc.sync, wbs_raw, wb_scales)
-        nc.sync.dma_start(wb_raw[:].bitcast(I32), wb_words[0].rearrange("p n t -> p (n t)").bitcast(I32))
-        nc.sync.dma_start(wa_raw[:].bitcast(I32), wa_words[0].bitcast(I32))
-        nc.sync.dma_start(tf_lo[:], tf_rows[:, 0:2, :])
+        nc.sync.dma_start(list_a[:], offs)
         nc.sync.dma_start(list_f[:], offs2)
-        load_scales_high(nc.sync, was_raw, wa_scales)
-        nc.sync.dma_start(tf_hi[:], tf_rows[:, 2:4, :])
+        nc.sync.dma_start(ob_sb[:], ob.rearrange("(p t) i -> p t i", t=PACK))
+        nc.sync.dma_start(wa_raw[:].bitcast(I32), wa_words[0].bitcast(I32))
+        nc.sync.dma_start(tf_mid[:], tf_rows[:, 2, :])
+        nc.sync.dma_start(tf_hi[:], tf_rows[:, 3, :])
         nc.sync.dma_start(bi_col[:], bi.rearrange("o (p c) -> p (o c)", c=2))
         load_scales_high(nc.gpsimd, wbs_raw, wb_scales)
-        load_scales_low(nc.gpsimd, was_raw, wa_scales)
+        load_scales_high(nc.gpsimd, was_raw, wa_scales)
 
         ones = tile("ones", [P, 32], F32)
         column = tile("column", [P, 32], F32)
@@ -94,12 +92,10 @@ def tile_list_meet_timestable_added_bundlemax_kernel(
             block = slice(32 * q, 32 * q + 32)
             nc.vector.tensor_tensor(ident[block, block], column[block, :], row[block, :], mybir.AluOpType.is_equal)
 
-        def gather_tokens(name, offsets, n):
-            words = tile(name + "_w", [P, n], U32)
-            scales = tile(name + "_s", [P, n], U8)
-            nc.vector.tensor_copy(words[:], xw[:].indirect(offsets[:]))
-            nc.vector.tensor_copy(scales[:], xs[:].indirect(offsets[:]))
-            return words, scales
+        def gather(name, window, offsets, dtype):
+            picked = tile(name, [P, J], dtype)
+            nc.vector.tensor_copy(picked[:], window[:].indirect(offsets[:]))
+            return picked
 
         def deal(copy, name, raw, dtype, run, tag=None):
             dealt = tile(name, [P, R], dtype, tag)
@@ -128,30 +124,24 @@ def tile_list_meet_timestable_added_bundlemax_kernel(
                 banks.append(bank)
             return banks
 
-        xb_w, xb_s = gather_tokens("xb", list_b, I)
-        xa_w, xa_s = gather_tokens("xa", list_a, J)
+        xb_w = gather("xb_w", xw, list_b, U32)
+        xb_s = gather("xb_s", xs, list_b, U8)
+        xa_w = gather("xa_w", xw, list_a, U32)
         wb_s = deal(nc.vector.tensor_copy, "wb_s", wbs_raw, U8, 16)
         wb_w = deal(nc.scalar.copy, "wb_w", wb_raw, U32, 4)
         zb = first_product("zb", wb_w, E5M2, wb_s, xb_w, xb_s)
-        wa_s = deal(nc.vector.tensor_copy, "wa_s", was_raw, U8, 16)
+        xa_s = gather("xa_s", xs, list_a, U8)
+        wa_s = deal(nc.vector.tensor_copy, "wa_s", was_raw, U8, 16, "wbs_raw")
         wa_w = deal(nc.scalar.copy, "wa_w", wa_raw, U16, 8)
         za = first_product("za", wa_w, E2M1, wa_s, xa_w, xa_s)
 
-        tfg = [tile(f"tfg{h}", [P, PACK, HALF], F32) for h in range(2)]
-        for pair, rows in enumerate((tf_lo, tf_hi)):
-            for h in range(2):
-                for u in range(2):
-                    nc.scalar.activation(
-                        tfg[h][:, 2 * pair + u, :], rows[:, u, :].indirect(list_f[:, 8 * h : 8 * h + 8]), COPY
-                    )
-
-        bias_ps = ps.tile([P, 2, P], F32, name="bias_ps")
-        for c in range(2):
-            nc.tensor.transpose(bias_ps[:, c, :], bi_col[:, c : c + 1].to_broadcast([P, P]), ident[:])
-        bias = tile("bias", [P, I], F32)
-        nc.scalar.activation(
-            bias[:].rearrange("p (n c) -> p n c", c=2), bias_ps[:].rearrange("p c n -> p n c"), COPY, scale=OUT_SCALE
-        )
+        tfg = tile("tfg", [P, PACK, J], F32)
+        for t, window in enumerate((tf_lo[:, 0, :], tf_lo[:, 1, :], tf_mid[:])):
+            nc.scalar.activation(tfg[:, t, :], window.indirect(list_f[:]), COPY)
+        for h in range(2):
+            nc.scalar.activation(
+                tfg[:, 3, h * HALF : (h + 1) * HALF], tf_hi[:].indirect(list_f[:, 8 * h : 8 * h + 8]), COPY
+            )
 
         def combine(dst, bank, other, op):
             nc.vector.tensor_tensor(
@@ -162,7 +152,7 @@ def tile_list_meet_timestable_added_bundlemax_kernel(
             )
 
         ha = [tile(f"ha{h}", [P, HALF * PACK], BF16) for h in range(2)]
-        hb = [tile("hb0", [P, HALF * PACK], BF16), tile("hb1", [P, HALF * PACK], BF16, tag="was_raw")]
+        hb = [tile(f"hb{h}", [P, HALF * PACK], BF16) for h in range(2)]
         ha_w = [tile(f"ha_w{h}", [P, HALF], U32) for h in range(2)]
         ha_s = [tile(f"ha_s{h}", [P, HALF], U8) for h in range(2)]
         hb_w = tile("hb_w", [P, I], U32)
@@ -173,9 +163,17 @@ def tile_list_meet_timestable_added_bundlemax_kernel(
             cols = slice(h * HALF, (h + 1) * HALF)
             nc.vector.quantize_mx(out=hb_w[:, cols].bitcast(E5M2), scales=hb_s[:, cols], in_=hb[h][:])
         for h in range(2):
-            combine(ha[h][:], za[h], tfg[h][:], MULT)
+            combine(ha[h][:], za[h], tfg[:, :, h * HALF : (h + 1) * HALF], MULT)
         for h in range(2):
             nc.vector.quantize_mx(out=ha_w[h][:].bitcast(E4M3), scales=ha_s[h][:], in_=ha[h][:])
+
+        bias_ps = ps.tile([P, 2, P], F32, name="bias_ps", tag="za0")
+        for c in range(2):
+            nc.tensor.transpose(bias_ps[:, c, :], bi_col[:, c : c + 1].to_broadcast([P, P]), ident[:])
+        bias = tile("bias", [P, I], F32)
+        nc.scalar.activation(
+            bias[:].rearrange("p (n c) -> p n c", c=2), bias_ps[:].rearrange("p c n -> p n c"), COPY, scale=OUT_SCALE
+        )
 
         scores = []
         for h in range(2):

@@ -69,8 +69,8 @@ def tile_list_meet_timestable_added_bundlemax_kernel(
         nc.sync.dma_start(list_b[:], offs3)
         nc.sync.dma_start(xw[:].bitcast(I32), xt_words[0].rearrange("p n t -> p (n t)").bitcast(I32))
         load_scales_low(nc.sync, xs, xt_scales)
-        load_scales_low(nc.sync, wbs_raw, wb_scales)
         nc.sync.dma_start(list_a[:], offs)
+        load_scales_low(nc.sync, wbs_raw, wb_scales)
         nc.sync.dma_start(list_f[:], offs2)
         nc.sync.dma_start(ob_sb[:], ob.rearrange("(p t) i -> p t i", t=PACK))
         nc.sync.dma_start(wa_raw[:].bitcast(I32), wa_words[0].bitcast(I32))
@@ -92,8 +92,8 @@ def tile_list_meet_timestable_added_bundlemax_kernel(
             block = slice(32 * q, 32 * q + 32)
             nc.vector.tensor_tensor(ident[block, block], column[block, :], row[block, :], mybir.AluOpType.is_equal)
 
-        def gather(name, window, offsets, dtype):
-            picked = tile(name, [P, J], dtype)
+        def gather(name, window, offsets, dtype, tag=None):
+            picked = tile(name, [P, J], dtype, tag)
             nc.vector.tensor_copy(picked[:], window[:].indirect(offsets[:]))
             return picked
 
@@ -130,8 +130,8 @@ def tile_list_meet_timestable_added_bundlemax_kernel(
         wb_s = deal(nc.vector.tensor_copy, "wb_s", wbs_raw, U8, 16)
         wb_w = deal(nc.scalar.copy, "wb_w", wb_raw, U32, 4)
         zb = first_product("zb", wb_w, E5M2, wb_s, xb_w, xb_s)
-        xa_s = gather("xa_s", xs, list_a, U8)
-        wa_s = deal(nc.vector.tensor_copy, "wa_s", was_raw, U8, 16, "wbs_raw")
+        xa_s = gather("xa_s", xs, list_a, U8, "wb_raw")
+        wa_s = deal(nc.gpsimd.tensor_copy, "wa_s", was_raw, U8, 16, "wbs_raw")
         wa_w = deal(nc.scalar.copy, "wa_w", wa_raw, U16, 8)
         za = first_product("za", wa_w, E2M1, wa_s, xa_w, xa_s)
 

from contextlib import ExitStack

import concourse.mybir as mybir

K, T, J, I, R, C, S = 512, 512, 256, 256, 512, 512, 32
FLOPS = 2 * K * R * J + 2 * K * R * I + 2 * R * J * I

F32 = mybir.dt.float32
BF16 = mybir.dt.bfloat16
I32 = mybir.dt.int32
U32 = mybir.dt.uint32
U16 = mybir.dt.uint16
U8 = mybir.dt.uint8
E4M3 = mybir.dt.float8_e4m3fn_x4
E5M2 = mybir.dt.float8_e5m2_x4
E2M1 = mybir.dt.float4_e2m1fn_x4
MULT = mybir.AluOpType.mult
ADD = mybir.AluOpType.add
MAX = mybir.AluOpType.max
COPY = mybir.ActivationFunctionType.Copy

P = 128
PACK = 4
HALF = 128
OUT_SCALE = 0.04


def tile_list_meet_timestable_added_bundlemax_kernel(
    tc, xt_words, xt_scales, wa_words, wa_scales, tf, wb_words, wb_scales, ob, bi, offs, offs2, offs3, out
):
    nc = tc.nc
    with ExitStack() as ctx:
        lists = ctx.enter_context(tc.tile_pool(name="lists", bufs=1))
        sb = ctx.enter_context(tc.tile_pool(name="sb", bufs=1))
        ps = ctx.enter_context(tc.psum_pool(name="ps", bufs=1))

        list_a = lists.tile([P, J // 16], U16, name="list_a")
        list_f = lists.tile([P, J // 16], U16, name="list_f")
        list_b = lists.tile([P, I // 16], U16, name="list_b")

        def tile(name, shape, dtype, tag=None):
            return sb.tile(shape, dtype, name=name, tag=tag or name, align_bytes=64)

        xw = tile("xw", [P, T], U32)
        xs = tile("xs", [P, T], U8)
        wa_raw = tile("wa_raw", [P, R], U16)
        was_raw = tile("was_raw", [P, R], U8)
        wb_raw = tile("wb_raw", [P, R], U32)
        wbs_raw = tile("wbs_raw", [P, R], U8)
        tf_lo = tile("tf_lo", [P, 2, C], F32)
        tf_mid = tile("tf_mid", [P, C], F32)
        tf_hi = tile("tf_hi", [P, C], F32)
        ob_sb = tile("ob_sb", [P, PACK, I], F32)
        bi_col = tile("bi_col", [P, 2], F32)

        def load_scales_low(queue, plane, scales):
            rows = scales[0, 0:4, :].bitcast(I32)
            queue.dma_start(plane[0:16, :].bitcast(I32), rows.unsqueeze(0).broadcast_to([4, 4, R // 4]))

        def load_scales_high(queue, plane, scales):
            rows = scales[0, 2:16, :].bitcast(I32)
            queue.dma_start(plane[16:P, :].bitcast(I32), rows.unsqueeze(0).broadcast_to([8, 14, R // 4]))

        tf_rows = tf.rearrange("(p t) c -> p t c", t=PACK)
        load_scales_low(nc.scalar, was_raw, wa_scales)
        load_scales_high(nc.scalar, xs, xt_scales)
        nc.scalar.dma_start(wb_raw[:].bitcast(I32), wb_words[0].rearrange("p n t -> p (n t)").bitcast(I32))
        nc.scalar.dma_start(tf_lo[:], tf_rows[:, 0:2, :])
        nc.sync.dma_start(list_b[:], offs3)
        nc.sync.dma_start(xw[:].bitcast(I32), xt_words[0].rearrange("p n t -> p (n t)").bitcast(I32))
        load_scales_low(nc.sync, xs, xt_scales)
        nc.sync.dma_start(list_a[:], offs)
        load_scales_low(nc.sync, wbs_raw, wb_scales)
        nc.sync.dma_start(list_f[:], offs2)
        nc.sync.dma_start(ob_sb[:], ob.rearrange("(p t) i -> p t i", t=PACK))
        nc.sync.dma_start(wa_raw[:].bitcast(I32), wa_words[0].bitcast(I32))
        nc.sync.dma_start(tf_mid[:], tf_rows[:, 2, :])
        nc.sync.dma_start(tf_hi[:], tf_rows[:, 3, :])
        nc.sync.dma_start(bi_col[:], bi.rearrange("o (p c) -> p (o c)", c=2))
        load_scales_high(nc.gpsimd, wbs_raw, wb_scales)
        load_scales_high(nc.gpsimd, was_raw, wa_scales)

        ones = tile("ones", [P, 32], F32)
        column = tile("column", [P, 32], F32)
        row = tile("row", [P, 32], F32)
        ident = tile("ident", [P, P], F32)
        nc.vector.memset(ones[:], 1.0)
        nc.vector.memset(ident[:], 0.0)
        nc.vector.tensor_tensor_scan(column[:], ones[:], ones[:], 0.0, MULT, ADD)
        nc.vector.transpose(row[:], column[:])
        for q in range(4):
            block = slice(32 * q, 32 * q + 32)
            nc.vector.tensor_tensor(ident[block, block], column[block, :], row[block, :], mybir.AluOpType.is_equal)

        def gather(name, window, offsets, dtype, tag=None):
            picked = tile(name, [P, J], dtype, tag)
            nc.vector.tensor_copy(picked[:], window[:].indirect(offsets[:]))
            return picked

        def deal(copy, name, raw, dtype, run, tag=None):
            dealt = tile(name, [P, R], dtype, tag)
            copy(
                dealt[:].rearrange("p (t c i) -> p c t i", t=PACK, i=run),
                raw[:].rearrange("p (c i t) -> p c t i", t=PACK, i=run),
            )
            return dealt

        def first_product(name, w_words, w_dtype, w_scales, x_words, x_scales):
            banks = []
            for h in range(2):
                bank = ps.tile([P, PACK, HALF], F32, name=f"{name}{h}")
                cols = slice(h * HALF, (h + 1) * HALF)
                for t in range(PACK):
                    rows = slice(t * P, (t + 1) * P)
                    nc.tensor.matmul_mx(
                        out=bank[:, t, :],
                        lhsT=w_words[:, rows].bitcast(w_dtype),
                        lhsT_scale=w_scales[:, rows],
                        rhs=x_words[:, cols].bitcast(E4M3),
                        rhs_scale=x_scales[:, cols],
                        start=True,
                        stop=True,
                    )
                banks.append(bank)
            return banks

        xb_w = gather("xb_w", xw, list_b, U32)
        xb_s = gather("xb_s", xs, list_b, U8)
        xa_w = gather("xa_w", xw, list_a, U32)
        wb_s = deal(nc.vector.tensor_copy, "wb_s", wbs_raw, U8, 16)
        wb_w = deal(nc.scalar.copy, "wb_w", wb_raw, U32, 4)
        zb = first_product("zb", wb_w, E5M2, wb_s, xb_w, xb_s)
        xa_s = gather("xa_s", xs, list_a, U8, "wb_raw")
        wa_s = deal(nc.gpsimd.tensor_copy, "wa_s", was_raw, U8, 16, "wbs_raw")
        wa_w = deal(nc.scalar.copy, "wa_w", wa_raw, U16, 8)
        za = first_product("za", wa_w, E2M1, wa_s, xa_w, xa_s)

        tfg = tile("tfg", [P, PACK, J], F32)
        for t, window in enumerate((tf_lo[:, 0, :], tf_lo[:, 1, :], tf_mid[:])):
            nc.scalar.activation(tfg[:, t, :], window.indirect(list_f[:]), COPY)
        for h in range(2):
            nc.scalar.activation(
                tfg[:, 3, h * HALF : (h + 1) * HALF], tf_hi[:].indirect(list_f[:, 8 * h : 8 * h + 8]), COPY
            )

        def combine(dst, bank, other, op):
            nc.vector.tensor_tensor(
                dst.rearrange("p (c i t) -> p c t i", t=PACK, i=2),
                bank[:].rearrange("p t (c i) -> p c t i", i=2),
                other.rearrange("p t (c i) -> p c t i", i=2),
                op,
            )

        ha = [tile(f"ha{h}", [P, HALF * PACK], BF16) for h in range(2)]
        hb = [tile(f"hb{h}", [P, HALF * PACK], BF16) for h in range(2)]
        ha_w = [tile(f"ha_w{h}", [P, HALF], U32) for h in range(2)]
        ha_s = [tile(f"ha_s{h}", [P, HALF], U8) for h in range(2)]
        hb_w = tile("hb_w", [P, I], U32)
        hb_s = tile("hb_s", [P, I], U8)
        for h in range(2):
            combine(hb[h][:], zb[h], ob_sb[:, :, h * HALF : (h + 1) * HALF], MAX)
        for h in range(2):
            cols = slice(h * HALF, (h + 1) * HALF)
            nc.vector.quantize_mx(out=hb_w[:, cols].bitcast(E5M2), scales=hb_s[:, cols], in_=hb[h][:])
        for h in range(2):
            combine(ha[h][:], za[h], tfg[:, :, h * HALF : (h + 1) * HALF], MULT)
        for h in range(2):
            nc.vector.quantize_mx(out=ha_w[h][:].bitcast(E4M3), scales=ha_s[h][:], in_=ha[h][:])

        bias_ps = ps.tile([P, 2, P], F32, name="bias_ps", tag="za0")
        for c in range(2):
            nc.tensor.transpose(bias_ps[:, c, :], bi_col[:, c : c + 1].to_broadcast([P, P]), ident[:])
        bias = tile("bias", [P, I], F32)
        nc.scalar.activation(
            bias[:].rearrange("p (n c) -> p n c", c=2), bias_ps[:].rearrange("p c n -> p n c"), COPY, scale=OUT_SCALE
        )

        scores = []
        for h in range(2):
            bank = ps.tile([P, I], F32, name=f"a0_{h}")
            nc.tensor.matmul_mx(
                out=bank[:],
                lhsT=ha_w[h][:].bitcast(E4M3),
                lhsT_scale=ha_s[h][:],
                rhs=hb_w[:].bitcast(E5M2),
                rhs_scale=hb_s[:],
                start=True,
                stop=True,
            )
            scored = tile(f"scored{h}", [P, I], F32)
            nc.vector.scalar_tensor_tensor(scored[:], bank[:], OUT_SCALE, bias[:], MULT, ADD)
            scores.append(scored)
        for h in range(2):
            best = tile(f"best{h}", [P, S], F32)
            nc.vector.tensor_reduce(
                best[:], scores[h][:].rearrange("p (s e) -> p s e", s=S), mybir.AxisListType.X, MAX
            )
            (nc.sync, nc.scalar)[h].dma_start(out[h * HALF : (h + 1) * HALF, :], best[:])
